import numpy as np
import ml_dtypes


def mxq(x, axis, fmt="e4m3"):
    dtype, down = {"e4m3": (ml_dtypes.float8_e4m3fn, 7), "e5m2": (ml_dtypes.float8_e5m2, 14)}[fmt]
    v = np.moveaxis(np.asarray(x, np.float32).astype(ml_dtypes.bfloat16).astype(np.float64), axis, -1)
    blocks = v.reshape(v.shape[:-1] + (-1, 32))
    amax = np.abs(blocks).max(-1, keepdims=True)
    byte = np.maximum(np.where(amax > 0, np.frexp(amax)[1] - 1 + 127, 0) - down, 1)
    scale = np.exp2(byte - 127.0)
    codes = (blocks / scale).astype(np.float32).astype(dtype).astype(np.float64)
    return np.moveaxis((codes * scale).reshape(v.shape), -1, axis)


WIDE = False


def mx_kscale(k):
    if not WIDE:
        return np.ones(k)
    levels = np.array([10, -10, 5, -5, 0])
    if k % 512:
        return np.exp2(np.random.permutation(np.resize(levels, k // 32))).repeat(32)
    a = np.empty((k // 512, 16))
    for p in range(k // 512):
        a[p, :8] = np.random.permutation(np.resize(levels, 8))
        for g in range(8):
            far = levels[np.abs(levels - a[p, g]) >= 10]
            a[p, g + 8] = far[np.random.randint(len(far))]
    return np.exp2(a.ravel()).repeat(32)


def f64(x):
    return np.asarray(x).astype(np.float64)


def striped(idx):
    return np.tile(np.asarray(idx).reshape(-1, 16).T, (8, 1)).astype(np.uint16)


def unstriped(offs):
    return offs[:16].T.reshape(-1).astype(np.int64)


E2M1 = np.array([0.0, 0.5, 1.0, 1.5, 2.0, 3.0, 4.0, 6.0, -0.0, -0.5, -1.0, -1.5, -2.0, -3.0, -4.0, -6.0])


def pack_weight(w, fmt):
    k, n = w.shape
    w = f64(np.asarray(w, np.float32).astype(ml_dtypes.bfloat16)).reshape(k // 32, 32, n)
    amax = np.abs(w).max(1)
    if fmt == "e4m3":
        byte = np.frexp(amax)[1] - 1 + 127 - 7
    else:
        mant, ex = np.frexp(amax / 6.0)
        byte = np.where(mant > 0.5, ex, ex - 1) + 127
    byte = np.clip(np.where(amax > 0, byte, 1), 1, 254)
    scaled = (w * np.exp2(127.0 - byte)[:, None, :]).reshape(k, n).astype(np.float32)
    by_word = np.ascontiguousarray(scaled.reshape(k // 512, 128, 4, n).transpose(0, 1, 3, 2))
    if fmt == "e4m3":
        words = by_word.astype(ml_dtypes.float8_e4m3fn).view(np.uint8)
    else:
        c = by_word.astype(ml_dtypes.float4_e2m1fn).view(np.uint8) & 0xF
        words = (c[..., 0::2] | (c[..., 1::2] << 4)).reshape(k // 512, 128, 2 * n)
    return np.ascontiguousarray(words), np.ascontiguousarray(byte.astype(np.uint8).reshape(k // 512, 16, n))


def unpack_weight(words, scales, fmt):
    g, _, n = scales.shape
    words = np.ascontiguousarray(words).reshape(g, 128, n, -1)
    if fmt == "e4m3":
        vals = words.view(ml_dtypes.float8_e4m3fn).astype(np.float64)
    else:
        nib = np.empty((g, 128, n, 4), np.uint8)
        nib[..., 0::2] = words & 0xF
        nib[..., 1::2] = words >> 4
        vals = E2M1[nib]
    vals = vals * np.repeat(np.exp2(scales.astype(np.float64) - 127.0), 8, axis=1)[..., None]
    return vals.transpose(0, 1, 3, 2).reshape(g * 512, n)


def bf(x):
    return np.asarray(x, np.float32).astype(ml_dtypes.bfloat16)


def planes(Y):
    r, m = Y.shape
    b = f64(bf(Y)).reshape(r // 32, 32, m)
    amax = np.abs(b).max(1)
    byte = np.clip(np.where(amax > 0, np.frexp(amax)[1] - 1 + 127 - 7, 1), 1, 254)
    codes = (b * np.exp2(127.0 - byte)[:, None, :]).reshape(r, m).astype(np.float32).astype(ml_dtypes.float8_e4m3fn).view(np.uint8)
    words = codes.reshape(r // 512, 128, 4, m).transpose(0, 1, 3, 2)
    return np.ascontiguousarray(words), np.ascontiguousarray(byte.astype(np.uint8).reshape(r // 512, 16, m))


C, I, T, N, L = 2048, 512, 512, 512, 512


def setup_inputs():
    n = np.random.standard_normal
    idx = np.random.permutation(C)[:I]
    fi = mx_kscale(I)
    fl = mx_kscale(L)
    ti = np.ones(C)
    ti[idx] = fi
    cxp = pack_weight(n((L, T)) / fl[:, None], "e4m3")
    wcp = pack_weight(n((L, N)) * 1 / np.sqrt(L) * fl[:, None], "e2m1")
    return {
        "xt": (n((T, C)) / ti).astype(np.float32),
        "wt": (n((N, C)) * (1 / np.sqrt(I)) * ti).astype(np.float32),
        "cx_words": cxp[0],
        "cx_scales": cxp[1],
        "wc_words": wcp[0],
        "wc_scales": wcp[1],
        "offs": striped(idx),
    }


def reference(xt, wt, cx_words, cx_scales, wc_words, wc_scales, offs):
    idx = unstriped(offs)
    cxu = unpack_weight(cx_words, cx_scales, "e4m3")
    wcu = unpack_weight(wc_words, wc_scales, "e2m1")
    xs = f64(xt)[:, idx].T
    ws1 = f64(wt)[:, idx].T
    ws1q = mxq(ws1, 0, "e4m3")
    xsq = mxq(xs, 0, "e4m3")
    y = ws1q.T @ xsq + wcu.T @ cxu
    words, scales = planes(y)
    return y, words, scales

@@ -1,0 +1,177 @@
+from contextlib import ExitStack
+
+import concourse.mybir as mybir
+from concourse.masks import make_identity
+
+C, I, T, N, L = 2048, 512, 512, 512, 512
+FLOPS = 2 * N * T * (I + L)
+
+F32 = mybir.dt.float32
+BF16 = mybir.dt.bfloat16
+I32 = mybir.dt.int32
+U32 = mybir.dt.uint32
+U16 = mybir.dt.uint16
+U8 = mybir.dt.uint8
+FP8X4 = mybir.dt.float8_e4m3fn_x4
+FP4X4 = mybir.dt.float4_e2m1fn_x4
+
+P = 128
+PACK = 4
+BLOCKS = T // P
+
+
+def tile_list_pruned_inputs_pl_kernel(tc, xt, wt, cx_words, cx_scales, wc_words, wc_scales, offs, out_0, out_1, out_2):
+    nc = tc.nc
+    with ExitStack() as ctx:
+        keep = ctx.enter_context(tc.tile_pool(name="keep", bufs=1))
+        ring = ctx.enter_context(tc.tile_pool(name="ring", bufs=2))
+        psum = ctx.enter_context(tc.psum_pool(name="psum", bufs=1))
+        psum2 = ctx.enter_context(tc.psum_pool(name="psum2", bufs=2))
+
+        offsets = keep.tile([P, I // 16], U16, name="offsets")
+        wc_raw = keep.tile([P, 2 * N], U8, name="wc_raw", align_bytes=64)
+        cx_codes = keep.tile([P, T], U32, name="cx_codes", align_bytes=64)
+        w_rows = [keep.tile([P, C], F32, name="w_rows%d" % r) for r in range(PACK)]
+        x_rows = [keep.tile([P, C], F32, name="x_rows%d" % j) for j in range(BLOCKS)]
+
+        wt_dealt = wt.rearrange("(p r) c -> r p c", r=PACK)
+        nc.sync.dma_start(wc_raw[:].bitcast(I32), wc_words[0].bitcast(I32))
+        nc.sync.dma_start(offsets[:], offs)
+        nc.sync.dma_start(w_rows[0][:], wt_dealt[0])
+        nc.sync.dma_start(cx_codes[:].bitcast(I32), cx_words[0].rearrange("p t r -> p (t r)").bitcast(I32))
+        for r in range(1, PACK):
+            nc.sync.dma_start(w_rows[r][:], wt_dealt[r])
+        for j in range(BLOCKS):
+            nc.sync.dma_start(x_rows[j][:], xt[j * P : (j + 1) * P, :])
+
+        wc_plane_raw = keep.tile([P, N], U8, name="wc_plane_raw", align_bytes=64)
+        cx_plane = keep.tile([P, T], U8, name="cx_plane", align_bytes=64)
+        for plane, scales in ((wc_plane_raw, wc_scales), (cx_plane, cx_scales)):
+            nc.gpsimd.memset(plane[:].bitcast(I32), 0)
+            for q in range(4):
+                nc.scalar.dma_start(plane[32 * q : 32 * q + 4, :].bitcast(I32), scales[0, 4 * q : 4 * q + 4, :].bitcast(I32))
+
+        identity = keep.tile([P, P], F32, name="identity")
+        make_identity(nc, identity[:])
+
+        wc_codes = keep.tile([P, 2 * N], U8, name="wc_codes", align_bytes=64)
+        wc_plane = keep.tile([P, N], U8, name="wc_plane", align_bytes=64)
+        nc.vector.tensor_copy(
+            wc_codes[:].rearrange("p (r m b) -> p r m b", r=PACK, b=2),
+            wc_raw[:].rearrange("p (m r b) -> p r m b", r=PACK, b=2),
+        )
+        nc.vector.tensor_copy(
+            wc_plane[:].rearrange("p (r m) -> p r m", r=PACK),
+            wc_plane_raw[:].rearrange("p (m r) -> p r m", r=PACK),
+        )
+
+        def pick_and_quantize(rows, name):
+            picked = ring.tile([P, I], BF16, name="picked", align_bytes=64)
+            nc.vector.tensor_copy(
+                picked[:].rearrange("p (u b e) -> p b u e", u=2, e=16),
+                rows[:].indirect(offsets[:]),
+            )
+            turned = psum2.tile([P, 2, P], F32, name="turned")
+            pairs = picked[:].bitcast(F32)
+            for u in range(2):
+                nc.tensor.transpose(turned[:, u, :], pairs[:, u * P : (u + 1) * P], identity[:])
+            grouped = ring.tile([P, PACK * P], BF16, name="grouped", align_bytes=64)
+            nc.scalar.copy(
+                grouped[:].bitcast(F32).rearrange("p (m u) -> p m u", u=2),
+                turned[:].rearrange("p u m -> p m u"),
+            )
+            codes = keep.tile([P, P], U32, name=name + "_codes", align_bytes=64)
+            plane = keep.tile([P, P], U8, name=name + "_plane", align_bytes=64)
+            nc.vector.quantize_mx(out=codes[:].bitcast(FP8X4), scales=plane[:], in_=grouped[:])
+            return codes, plane
+
+        def context_pass(acc, r, j, start):
+            cols = slice(j * P, (j + 1) * P)
+            nc.tensor.matmul_mx(
+                out=acc,
+                lhsT=wc_codes[:, 2 * P * r : 2 * P * (r + 1)].bitcast(FP4X4),
+                lhsT_scale=wc_plane[:, P * r : P * (r + 1)],
+                rhs=cx_codes[:, cols].bitcast(FP8X4),
+                rhs_scale=cx_plane[:, cols],
+                start=start,
+                stop=False,
+            )
+
+        def picked_pass(acc, w_mx, x_mx, stop):
+            nc.tensor.matmul_mx(
+                out=acc,
+                lhsT=w_mx[0][:].bitcast(FP8X4),
+                lhsT_scale=w_mx[1][:],
+                rhs=x_mx[0][:].bitcast(FP8X4),
+                rhs_scale=x_mx[1][:],
+                start=False,
+                stop=stop,
+            )
+
+        y_codes = keep.tile([P, T], U32, name="y_codes", align_bytes=64)
+        y_plane = keep.tile([P, T], U8, name="y_plane", align_bytes=64)
+        y_first = keep.tile([P, PACK, 2 * P], F32, name="y_first")
+        y_third = keep.tile([P, PACK, P], F32, name="y_third")
+        y_last = keep.tile([P, PACK, P], F32, name="y_last")
+        out_rows = out_0.rearrange("(p r) t -> p r t", r=PACK)
+        out_words = out_1[0].rearrange("p t r -> p (t r)").bitcast(I32)
+
+        def quantize_result(y_grouped, j):
+            cols = slice(j * P, (j + 1) * P)
+            nc.vector.quantize_mx(out=y_codes[:, cols].bitcast(FP8X4), scales=y_plane[:, cols], in_=y_grouped[:])
+
+        def group_from_sbuf(y_sbuf):
+            y_grouped = ring.tile([P, PACK * P], BF16, name="y_grouped", align_bytes=64)
+            nc.vector.tensor_copy(
+                y_grouped[:].rearrange("p (c i r) -> p c r i", i=4, r=PACK),
+                y_sbuf[:].rearrange("p r (c i) -> p c r i", i=4),
+            )
+            return y_grouped
+
+        w_mx = [pick_and_quantize(w_rows[r], "w%d" % r) for r in range(PACK)]
+
+        last_banks = [psum.tile([P, P], F32, name="last%d" % r) for r in range(PACK)]
+        for r in range(PACK):
+            context_pass(last_banks[r][:], r, BLOCKS - 1, True)
+
+        def open_bank(j):
+            bank = psum2.tile([P, PACK, P], F32, name="bank")
+            for r in range(PACK):
+                context_pass(bank[:, r, :], r, j, r == 0)
+            return bank
+
+        def close_bank(bank, x_mx):
+            for r in range(PACK):
+                picked_pass(bank[:, r, :], w_mx[r], x_mx, r == PACK - 1)
+
+        for j in range(2):
+            bank = open_bank(j)
+            x_mx = pick_and_quantize(x_rows[j], "x%d" % j)
+            close_bank(bank, x_mx)
+            nc.scalar.copy(y_first[:, :, j * P : (j + 1) * P], bank[:])
+            y_grouped = ring.tile([P, PACK * P], BF16, name="y_grouped", align_bytes=64)
+            nc.scalar.copy(y_grouped[:].rearrange("p (t r) -> p t r", r=PACK), bank[:].rearrange("p r t -> p t r"))
+            quantize_result(y_grouped, j)
+        nc.sync.dma_start(out_rows[:, :, 0 : 2 * P], y_first[:])
+
+        bank = open_bank(2)
+        x_mx = pick_and_quantize(x_rows[2], "x2")
+        close_bank(bank, x_mx)
+        nc.scalar.copy(y_third[:], bank[:])
+        nc.sync.dma_start(out_rows[:, :, 2 * P : 3 * P], y_third[:])
+
+        x_mx = pick_and_quantize(x_rows[3], "x3")
+        quantize_result(group_from_sbuf(y_third), 2)
+        nc.sync.dma_start(out_words[:, 0 : 3 * P], y_codes[:, 0 : 3 * P].bitcast(I32))
+        for r in range(PACK):
+            picked_pass(last_banks[r][:], w_mx[r], x_mx, True)
+            if r % 2 == 0:
+                nc.scalar.copy(y_last[:, r, :], last_banks[r][:])
+            else:
+                nc.vector.tensor_copy(y_last[:, r, :], last_banks[r][:])
+        nc.scalar.dma_start(out_rows[:, :, 3 * P : 4 * P], y_last[:])
+        quantize_result(group_from_sbuf(y_last), 3)
+        nc.sync.dma_start(out_words[:, 3 * P : 4 * P], y_codes[:, 3 * P : 4 * P].bitcast(I32))
+        for q in range(4):
+            queue = nc.sync if q < 2 else nc.scalar
+            queue.dma_start(out_2[0, 4 * q : 4 * q + 4, :].bitcast(I32), y_plane[32 * q : 32 * q + 4, :].bitcast(I32))

@@ -18,6 +18,7 @@ FP4X4 = mybir.dt.float4_e2m1fn_x4
 P = 128
 PACK = 4
 BLOCKS = T // P
+ROW_BYTES = 4 * C
 
 
 def tile_list_pruned_inputs_pl_kernel(tc, xt, wt, cx_words, cx_scales, wc_words, wc_scales, offs, out_0, out_1, out_2):
@@ -26,52 +27,56 @@ def tile_list_pruned_inputs_pl_kernel(tc, xt, wt, cx_words, cx_scales, wc_words,
         keep = ctx.enter_context(tc.tile_pool(name="keep", bufs=1))
         ring = ctx.enter_context(tc.tile_pool(name="ring", bufs=2))
         psum = ctx.enter_context(tc.psum_pool(name="psum", bufs=1))
-        psum2 = ctx.enter_context(tc.psum_pool(name="psum2", bufs=2))
+        rows = ctx.enter_context(tc.tile_pool(name="rows", bufs=1))
 
         offsets = keep.tile([P, I // 16], U16, name="offsets")
         wc_raw = keep.tile([P, 2 * N], U8, name="wc_raw", align_bytes=64)
         cx_codes = keep.tile([P, T], U32, name="cx_codes", align_bytes=64)
-        w_rows = [keep.tile([P, C], F32, name="w_rows%d" % r) for r in range(PACK)]
-        x_rows = [keep.tile([P, C], F32, name="x_rows%d" % j) for j in range(BLOCKS)]
+        windows = [rows.tile([P, C], F32, name="window%d" % i, offset=i * ROW_BYTES, align_bytes=64) for i in range(2 * PACK)]
+        w_rows = windows[:PACK]
+        x_rows = windows[PACK:]
+
+        def over_window(i, at, shape, dtype, name):
+            return rows.tile(shape, dtype, name=name, offset=i * ROW_BYTES + at, align_bytes=64)
+
+        wc_plane_raw = keep.tile([P, N], U8, name="wc_plane_raw", align_bytes=64)
+        cx_plane = keep.tile([P, T], U8, name="cx_plane", align_bytes=64)
+        nc.gpsimd.memset(wc_plane_raw[:].bitcast(I32), 0)
+        nc.gpsimd.memset(cx_plane[:].bitcast(I32), 0)
+
+        def load_scale_rows(plane, scales):
+            for q in range(4):
+                nc.sync.dma_start(plane[32 * q : 32 * q + 4, :].bitcast(I32), scales[0, 4 * q : 4 * q + 4, :].bitcast(I32))
 
         wt_dealt = wt.rearrange("(p r) c -> r p c", r=PACK)
         nc.sync.dma_start(wc_raw[:].bitcast(I32), wc_words[0].bitcast(I32))
         nc.sync.dma_start(offsets[:], offs)
         nc.sync.dma_start(w_rows[0][:], wt_dealt[0])
+        nc.sync.dma_start(w_rows[1][:], wt_dealt[1])
+        load_scale_rows(wc_plane_raw, wc_scales)
         nc.sync.dma_start(cx_codes[:].bitcast(I32), cx_words[0].rearrange("p t r -> p (t r)").bitcast(I32))
-        for r in range(1, PACK):
-            nc.sync.dma_start(w_rows[r][:], wt_dealt[r])
+        nc.sync.dma_start(w_rows[2][:], wt_dealt[2])
+        load_scale_rows(cx_plane, cx_scales)
+        nc.sync.dma_start(w_rows[3][:], wt_dealt[3])
         for j in range(BLOCKS):
             nc.sync.dma_start(x_rows[j][:], xt[j * P : (j + 1) * P, :])
-
-        wc_plane_raw = keep.tile([P, N], U8, name="wc_plane_raw", align_bytes=64)
-        cx_plane = keep.tile([P, T], U8, name="cx_plane", align_bytes=64)
-        for plane, scales in ((wc_plane_raw, wc_scales), (cx_plane, cx_scales)):
-            nc.gpsimd.memset(plane[:].bitcast(I32), 0)
-            for q in range(4):
-                nc.scalar.dma_start(plane[32 * q : 32 * q + 4, :].bitcast(I32), scales[0, 4 * q : 4 * q + 4, :].bitcast(I32))
 
         identity = keep.tile([P, P], F32, name="identity")
         make_identity(nc, identity[:])
 
         wc_codes = keep.tile([P, 2 * N], U8, name="wc_codes", align_bytes=64)
-        wc_plane = keep.tile([P, N], U8, name="wc_plane", align_bytes=64)
         nc.vector.tensor_copy(
             wc_codes[:].rearrange("p (r m b) -> p r m b", r=PACK, b=2),
             wc_raw[:].rearrange("p (m r b) -> p r m b", r=PACK, b=2),
         )
-        nc.vector.tensor_copy(
-            wc_plane[:].rearrange("p (r m) -> p r m", r=PACK),
-            wc_plane_raw[:].rearrange("p (m r) -> p r m", r=PACK),
-        )
 
-        def pick_and_quantize(rows, name):
+        def pick(i):
             picked = ring.tile([P, I], BF16, name="picked", align_bytes=64)
             nc.vector.tensor_copy(
                 picked[:].rearrange("p (u b e) -> p b u e", u=2, e=16),
-                rows[:].indirect(offsets[:]),
+                windows[i][:].indirect(offsets[:]),
             )
-            turned = psum2.tile([P, 2, P], F32, name="turned")
+            turned = psum.tile([P, 2, P], F32, name="turned")
             pairs = picked[:].bitcast(F32)
             for u in range(2):
                 nc.tensor.transpose(turned[:, u, :], pairs[:, u * P : (u + 1) * P], identity[:])
@@ -80,10 +85,18 @@ def tile_list_pruned_inputs_pl_kernel(tc, xt, wt, cx_words, cx_scales, wc_words,
                 grouped[:].bitcast(F32).rearrange("p (m u) -> p m u", u=2),
                 turned[:].rearrange("p u m -> p m u"),
             )
-            codes = keep.tile([P, P], U32, name=name + "_codes", align_bytes=64)
-            plane = keep.tile([P, P], U8, name=name + "_plane", align_bytes=64)
+            return grouped
+
+        def quantize(grouped, i, held):
+            if held:
+                codes = over_window(i + 1, 0, [P, P], U32, "codes%d" % i)
+            else:
+                codes = keep.tile([P, P], U32, name="codes%d" % i, align_bytes=64)
+            plane = keep.tile([P, P], U8, name="plane%d" % i, align_bytes=64)
             nc.vector.quantize_mx(out=codes[:].bitcast(FP8X4), scales=plane[:], in_=grouped[:])
             return codes, plane
+
+        wc_plane = over_window(2, 1024, [P, N], U8, "wc_plane")
 
         def context_pass(acc, r, j, start):
             cols = slice(j * P, (j + 1) * P)
@@ -108,70 +121,80 @@ def tile_list_pruned_inputs_pl_kernel(tc, xt, wt, cx_words, cx_scales, wc_words,
                 stop=stop,
             )
 
-        y_codes = keep.tile([P, T], U32, name="y_codes", align_bytes=64)
         y_plane = keep.tile([P, T], U8, name="y_plane", align_bytes=64)
-        y_first = keep.tile([P, PACK, 2 * P], F32, name="y_first")
-        y_third = keep.tile([P, PACK, P], F32, name="y_third")
-        y_last = keep.tile([P, PACK, P], F32, name="y_last")
+        y_first = [keep.tile([P, PACK, P], F32, name="y_first%d" % j) for j in range(2)]
         out_rows = out_0.rearrange("(p r) t -> p r t", r=PACK)
         out_words = out_1[0].rearrange("p t r -> p (t r)").bitcast(I32)
 
-        def quantize_result(y_grouped, j):
-            cols = slice(j * P, (j + 1) * P)
-            nc.vector.quantize_mx(out=y_codes[:, cols].bitcast(FP8X4), scales=y_plane[:, cols], in_=y_grouped[:])
+        def quantize_result(y_codes, y_grouped, cols, queue):
+            nc.vector.quantize_mx(out=y_codes[:].bitcast(FP8X4), scales=y_plane[:, cols], in_=y_grouped[:])
+            queue.dma_start(out_words[:, cols], y_codes[:].bitcast(I32))
 
-        def group_from_sbuf(y_sbuf):
-            y_grouped = ring.tile([P, PACK * P], BF16, name="y_grouped", align_bytes=64)
-            nc.vector.tensor_copy(
-                y_grouped[:].rearrange("p (c i r) -> p c r i", i=4, r=PACK),
-                y_sbuf[:].rearrange("p r (c i) -> p c r i", i=4),
-            )
-            return y_grouped
+        def group_from_bank(y_grouped, bank):
+            nc.scalar.copy(y_grouped.rearrange("p (t r) -> p t r", r=PACK), bank[:].rearrange("p r t -> p t r"))
 
-        w_mx = [pick_and_quantize(w_rows[r], "w%d" % r) for r in range(PACK)]
+        banks = [psum.tile([P, PACK, P], F32, name="bank%d" % j) for j in range(BLOCKS - 1)]
+        last_banks = [psum.tile([P, 2, P], F32, name="last%d" % h) for h in range(2)]
 
-        last_banks = [psum.tile([P, P], F32, name="last%d" % r) for r in range(PACK)]
-        for r in range(PACK):
-            context_pass(last_banks[r][:], r, BLOCKS - 1, True)
-
-        def open_bank(j):
-            bank = psum2.tile([P, PACK, P], F32, name="bank")
+        def close_bank(j, x_mx):
             for r in range(PACK):
-                context_pass(bank[:, r, :], r, j, r == 0)
-            return bank
+                picked_pass(banks[j][:, r, :], mx[r], x_mx, r == PACK - 1)
 
-        def close_bank(bank, x_mx):
-            for r in range(PACK):
-                picked_pass(bank[:, r, :], w_mx[r], x_mx, r == PACK - 1)
+        grouped_first = keep.tile([P, 2 * PACK * P], BF16, name="grouped_first", align_bytes=64)
+        mx = []
+        grouped = [pick(0)]
+        for i in range(1, 7):
+            grouped.append(pick(i))
+            mx.append(quantize(grouped[i - 1], i - 1, True))
+            if i == 2:
+                nc.vector.tensor_copy(
+                    wc_plane[:].rearrange("p (r m) -> p r m", r=PACK),
+                    wc_plane_raw[:].rearrange("p (m r) -> p r m", r=PACK),
+                )
+                for j in range(BLOCKS - 1):
+                    for r in range(PACK):
+                        context_pass(banks[j][:, r, :], r, j, r == 0)
+                for r in range(PACK):
+                    context_pass(last_banks[r // 2][:, r % 2, :], r, BLOCKS - 1, r % 2 == 0)
+            if i > PACK:
+                j = i - 1 - PACK
+                close_bank(j, mx[i - 1])
+                nc.scalar.copy(y_first[j][:], banks[j][:])
+                nc.sync.dma_start(out_rows[:, :, j * P : (j + 1) * P], y_first[j][:])
+                group_from_bank(grouped_first[:, j * PACK * P : (j + 1) * PACK * P], banks[j])
 
-        for j in range(2):
-            bank = open_bank(j)
-            x_mx = pick_and_quantize(x_rows[j], "x%d" % j)
-            close_bank(bank, x_mx)
-            nc.scalar.copy(y_first[:, :, j * P : (j + 1) * P], bank[:])
-            y_grouped = ring.tile([P, PACK * P], BF16, name="y_grouped", align_bytes=64)
-            nc.scalar.copy(y_grouped[:].rearrange("p (t r) -> p t r", r=PACK), bank[:].rearrange("p r t -> p t r"))
-            quantize_result(y_grouped, j)
-        nc.sync.dma_start(out_rows[:, :, 0 : 2 * P], y_first[:])
-
-        bank = open_bank(2)
-        x_mx = pick_and_quantize(x_rows[2], "x2")
-        close_bank(bank, x_mx)
-        nc.scalar.copy(y_third[:], bank[:])
+        grouped.append(pick(7))
+        mx.append(quantize(grouped[6], 6, True))
+        close_bank(2, mx[6])
+        codes_first = over_window(7, 2048, [P, 2 * P], U32, "codes_first")
+        quantize_result(codes_first, grouped_first, slice(0, 2 * P), nc.sync)
+        mx.append(quantize(grouped[7], 7, False))
+        y_third = keep.tile([P, PACK, P], F32, name="y_third")
+        nc.scalar.copy(y_third[:], banks[2][:])
         nc.sync.dma_start(out_rows[:, :, 2 * P : 3 * P], y_third[:])
+        grouped_third = keep.tile([P, PACK * P], BF16, name="grouped_third", align_bytes=64)
+        nc.vector.tensor_copy(
+            grouped_third[:].rearrange("p (c i r) -> p c r i", i=4, r=PACK),
+            y_third[:].rearrange("p r (c i) -> p c r i", i=4),
+        )
+        codes_third = keep.tile([P, P], U32, name="codes_third", align_bytes=64)
+        quantize_result(codes_third, grouped_third, slice(2 * P, 3 * P), nc.sync)
 
-        x_mx = pick_and_quantize(x_rows[3], "x3")
-        quantize_result(group_from_sbuf(y_third), 2)
-        nc.sync.dma_start(out_words[:, 0 : 3 * P], y_codes[:, 0 : 3 * P].bitcast(I32))
-        for r in range(PACK):
-            picked_pass(last_banks[r][:], w_mx[r], x_mx, True)
-            if r % 2 == 0:
-                nc.scalar.copy(y_last[:, r, :], last_banks[r][:])
-            else:
-                nc.vector.tensor_copy(y_last[:, r, :], last_banks[r][:])
-        nc.scalar.dma_start(out_rows[:, :, 3 * P : 4 * P], y_last[:])
-        quantize_result(group_from_sbuf(y_last), 3)
-        nc.sync.dma_start(out_words[:, 3 * P : 4 * P], y_codes[:, 3 * P : 4 * P].bitcast(I32))
+        grouped_last = keep.tile([P, PACK * P], BF16, name="grouped_last", align_bytes=64)
+        y_last = [keep.tile([P, 2, P], F32, name="y_last%d" % h) for h in range(2)]
+        for h in range(2):
+            for e in range(2):
+                picked_pass(last_banks[h][:, e, :], mx[2 * h + e], mx[7], e == 1)
+            nc.scalar.copy(
+                grouped_last[:].rearrange("p (t h e) -> p h t e", h=2, e=2)[:, h, :, :],
+                last_banks[h][:].rearrange("p e t -> p t e"),
+            )
+        nc.vector.tensor_copy(y_last[0][:], last_banks[0][:])
+        nc.sync.dma_start(out_rows[:, 0:2, 3 * P : 4 * P], y_last[0][:])
+        codes_last = keep.tile([P, P], U32, name="codes_last", align_bytes=64)
+        quantize_result(codes_last, grouped_last, slice(3 * P, 4 * P), nc.sync)
+        nc.scalar.copy(y_last[1][:], last_banks[1][:])
+        nc.scalar.dma_start(out_rows[:, 2:4, 3 * P : 4 * P], y_last[1][:])
         for q in range(4):
             queue = nc.sync if q < 2 else nc.scalar
             queue.dma_start(out_2[0, 4 * q : 4 * q + 4, :].bitcast(I32), y_plane[32 * q : 32 * q + 4, :].bitcast(I32))

from contextlib import ExitStack

import concourse.mybir as mybir
from concourse.masks import make_identity

C, I, T, N, L = 2048, 512, 512, 512, 512
FLOPS = 2 * N * T * (I + L)

F32 = mybir.dt.float32
BF16 = mybir.dt.bfloat16
I32 = mybir.dt.int32
U32 = mybir.dt.uint32
U16 = mybir.dt.uint16
U8 = mybir.dt.uint8
FP8X4 = mybir.dt.float8_e4m3fn_x4
FP4X4 = mybir.dt.float4_e2m1fn_x4

P = 128
PACK = 4
BLOCKS = T // P
ROW_BYTES = 4 * C


def tile_list_pruned_inputs_pl_kernel(tc, xt, wt, cx_words, cx_scales, wc_words, wc_scales, offs, out_0, out_1, out_2):
    nc = tc.nc
    with ExitStack() as ctx:
        keep = ctx.enter_context(tc.tile_pool(name="keep", bufs=1))
        ring = ctx.enter_context(tc.tile_pool(name="ring", bufs=2))
        psum = ctx.enter_context(tc.psum_pool(name="psum", bufs=1))
        rows = ctx.enter_context(tc.tile_pool(name="rows", bufs=1))

        offsets = keep.tile([P, I // 16], U16, name="offsets")
        wc_raw = keep.tile([P, 2 * N], U8, name="wc_raw", align_bytes=64)
        cx_codes = keep.tile([P, T], U32, name="cx_codes", align_bytes=64)
        windows = [rows.tile([P, C], F32, name="window%d" % i, offset=i * ROW_BYTES, align_bytes=64) for i in range(2 * PACK)]
        w_rows = windows[:PACK]
        x_rows = windows[PACK:]

        def over_window(i, at, shape, dtype, name):
            return rows.tile(shape, dtype, name=name, offset=i * ROW_BYTES + at, align_bytes=64)

        wc_plane_raw = keep.tile([P, N], U8, name="wc_plane_raw", align_bytes=64)
        cx_plane = keep.tile([P, T], U8, name="cx_plane", align_bytes=64)
        nc.gpsimd.memset(wc_plane_raw[:].bitcast(I32), 0)
        nc.gpsimd.memset(cx_plane[:].bitcast(I32), 0)

        def load_scale_rows(plane, scales):
            for q in range(4):
                nc.sync.dma_start(plane[32 * q : 32 * q + 4, :].bitcast(I32), scales[0, 4 * q : 4 * q + 4, :].bitcast(I32))

        wt_dealt = wt.rearrange("(p r) c -> r p c", r=PACK)
        nc.sync.dma_start(wc_raw[:].bitcast(I32), wc_words[0].bitcast(I32))
        nc.sync.dma_start(offsets[:], offs)
        nc.sync.dma_start(w_rows[0][:], wt_dealt[0])
        nc.sync.dma_start(w_rows[1][:], wt_dealt[1])
        load_scale_rows(wc_plane_raw, wc_scales)
        nc.sync.dma_start(cx_codes[:].bitcast(I32), cx_words[0].rearrange("p t r -> p (t r)").bitcast(I32))
        nc.sync.dma_start(w_rows[2][:], wt_dealt[2])
        load_scale_rows(cx_plane, cx_scales)
        nc.sync.dma_start(w_rows[3][:], wt_dealt[3])
        for j in range(BLOCKS):
            nc.sync.dma_start(x_rows[j][:], xt[j * P : (j + 1) * P, :])

        identity = keep.tile([P, P], F32, name="identity")
        make_identity(nc, identity[:])

        wc_codes = keep.tile([P, 2 * N], U8, name="wc_codes", align_bytes=64)
        nc.vector.tensor_copy(
            wc_codes[:].rearrange("p (r m b) -> p r m b", r=PACK, b=2),
            wc_raw[:].rearrange("p (m r b) -> p r m b", r=PACK, b=2),
        )

        def pick(i):
            picked = ring.tile([P, I], BF16, name="picked", align_bytes=64)
            nc.vector.tensor_copy(
                picked[:].rearrange("p (u b e) -> p b u e", u=2, e=16),
                windows[i][:].indirect(offsets[:]),
            )
            turned = psum.tile([P, 2, P], F32, name="turned")
            pairs = picked[:].bitcast(F32)
            for u in range(2):
                nc.tensor.transpose(turned[:, u, :], pairs[:, u * P : (u + 1) * P], identity[:])
            grouped = ring.tile([P, PACK * P], BF16, name="grouped", align_bytes=64)
            nc.scalar.copy(
                grouped[:].bitcast(F32).rearrange("p (m u) -> p m u", u=2),
                turned[:].rearrange("p u m -> p m u"),
            )
            return grouped

        def quantize(grouped, i, held):
            if held:
                codes = over_window(i + 1, 0, [P, P], U32, "codes%d" % i)
            else:
                codes = keep.tile([P, P], U32, name="codes%d" % i, align_bytes=64)
            plane = keep.tile([P, P], U8, name="plane%d" % i, align_bytes=64)
            nc.vector.quantize_mx(out=codes[:].bitcast(FP8X4), scales=plane[:], in_=grouped[:])
            return codes, plane

        wc_plane = over_window(2, 1024, [P, N], U8, "wc_plane")

        def context_pass(acc, r, j, start):
            cols = slice(j * P, (j + 1) * P)
            nc.tensor.matmul_mx(
                out=acc,
                lhsT=wc_codes[:, 2 * P * r : 2 * P * (r + 1)].bitcast(FP4X4),
                lhsT_scale=wc_plane[:, P * r : P * (r + 1)],
                rhs=cx_codes[:, cols].bitcast(FP8X4),
                rhs_scale=cx_plane[:, cols],
                start=start,
                stop=False,
            )

        def picked_pass(acc, w_mx, x_mx, stop):
            nc.tensor.matmul_mx(
                out=acc,
                lhsT=w_mx[0][:].bitcast(FP8X4),
                lhsT_scale=w_mx[1][:],
                rhs=x_mx[0][:].bitcast(FP8X4),
                rhs_scale=x_mx[1][:],
                start=False,
                stop=stop,
            )

        y_plane = keep.tile([P, T], U8, name="y_plane", align_bytes=64)
        y_first = [keep.tile([P, PACK, P], F32, name="y_first%d" % j) for j in range(2)]
        out_rows = out_0.rearrange("(p r) t -> p r t", r=PACK)
        out_words = out_1[0].rearrange("p t r -> p (t r)").bitcast(I32)

        def quantize_result(y_codes, y_grouped, cols, queue):
            nc.vector.quantize_mx(out=y_codes[:].bitcast(FP8X4), scales=y_plane[:, cols], in_=y_grouped[:])
            queue.dma_start(out_words[:, cols], y_codes[:].bitcast(I32))

        def group_from_bank(y_grouped, bank):
            nc.scalar.copy(y_grouped.rearrange("p (t r) -> p t r", r=PACK), bank[:].rearrange("p r t -> p t r"))

        banks = [psum.tile([P, PACK, P], F32, name="bank%d" % j) for j in range(BLOCKS - 1)]
        last_banks = [psum.tile([P, 2, P], F32, name="last%d" % h) for h in range(2)]

        def close_bank(j, x_mx):
            for r in range(PACK):
                picked_pass(banks[j][:, r, :], mx[r], x_mx, r == PACK - 1)

        grouped_first = keep.tile([P, 2 * PACK * P], BF16, name="grouped_first", align_bytes=64)
        mx = []
        grouped = [pick(0)]
        for i in range(1, 7):
            grouped.append(pick(i))
            mx.append(quantize(grouped[i - 1], i - 1, True))
            if i == 2:
                nc.vector.tensor_copy(
                    wc_plane[:].rearrange("p (r m) -> p r m", r=PACK),
                    wc_plane_raw[:].rearrange("p (m r) -> p r m", r=PACK),
                )
                for j in range(BLOCKS - 1):
                    for r in range(PACK):
                        context_pass(banks[j][:, r, :], r, j, r == 0)
                for r in range(PACK):
                    context_pass(last_banks[r // 2][:, r % 2, :], r, BLOCKS - 1, r % 2 == 0)
            if i > PACK:
                j = i - 1 - PACK
                close_bank(j, mx[i - 1])
                nc.scalar.copy(y_first[j][:], banks[j][:])
                nc.sync.dma_start(out_rows[:, :, j * P : (j + 1) * P], y_first[j][:])
                group_from_bank(grouped_first[:, j * PACK * P : (j + 1) * PACK * P], banks[j])

        grouped.append(pick(7))
        mx.append(quantize(grouped[6], 6, True))
        close_bank(2, mx[6])
        codes_first = over_window(7, 2048, [P, 2 * P], U32, "codes_first")
        quantize_result(codes_first, grouped_first, slice(0, 2 * P), nc.sync)
        mx.append(quantize(grouped[7], 7, False))
        y_third = keep.tile([P, PACK, P], F32, name="y_third")
        nc.scalar.copy(y_third[:], banks[2][:])
        nc.sync.dma_start(out_rows[:, :, 2 * P : 3 * P], y_third[:])
        grouped_third = keep.tile([P, PACK * P], BF16, name="grouped_third", align_bytes=64)
        nc.vector.tensor_copy(
            grouped_third[:].rearrange("p (c i r) -> p c r i", i=4, r=PACK),
            y_third[:].rearrange("p r (c i) -> p c r i", i=4),
        )
        codes_third = keep.tile([P, P], U32, name="codes_third", align_bytes=64)
        quantize_result(codes_third, grouped_third, slice(2 * P, 3 * P), nc.sync)

        grouped_last = keep.tile([P, PACK * P], BF16, name="grouped_last", align_bytes=64)
        y_last = [keep.tile([P, 2, P], F32, name="y_last%d" % h) for h in range(2)]
        for h in range(2):
            for e in range(2):
                picked_pass(last_banks[h][:, e, :], mx[2 * h + e], mx[7], e == 1)
            nc.scalar.copy(
                grouped_last[:].rearrange("p (t h e) -> p h t e", h=2, e=2)[:, h, :, :],
                last_banks[h][:].rearrange("p e t -> p t e"),
            )
        nc.vector.tensor_copy(y_last[0][:], last_banks[0][:])
        nc.sync.dma_start(out_rows[:, 0:2, 3 * P : 4 * P], y_last[0][:])
        codes_last = keep.tile([P, P], U32, name="codes_last", align_bytes=64)
        quantize_result(codes_last, grouped_last, slice(3 * P, 4 * P), nc.sync)
        nc.scalar.copy(y_last[1][:], last_banks[1][:])
        nc.scalar.dma_start(out_rows[:, 2:4, 3 * P : 4 * P], y_last[1][:])
        for q in range(4):
            queue = nc.sync if q < 2 else nc.scalar
            queue.dma_start(out_2[0, 4 * q : 4 * q + 4, :].bitcast(I32), y_plane[32 * q : 32 * q + 4, :].bitcast(I32))
